import numpy as np
import ml_dtypes


def mxq(x, axis, fmt="e4m3"):
    dtype, down = {"e4m3": (ml_dtypes.float8_e4m3fn, 7), "e5m2": (ml_dtypes.float8_e5m2, 14)}[fmt]
    v = np.moveaxis(np.asarray(x, np.float32).astype(ml_dtypes.bfloat16).astype(np.float64), axis, -1)
    blocks = v.reshape(v.shape[:-1] + (-1, 32))
    amax = np.abs(blocks).max(-1, keepdims=True)
    byte = np.maximum(np.where(amax > 0, np.frexp(amax)[1] - 1 + 127, 0) - down, 1)
    scale = np.exp2(byte - 127.0)
    codes = (blocks / scale).astype(np.float32).astype(dtype).astype(np.float64)
    return np.moveaxis((codes * scale).reshape(v.shape), -1, axis)


WIDE = False


def mx_kscale(k):
    if not WIDE:
        return np.ones(k)
    levels = np.array([10, -10, 5, -5, 0])
    if k % 512:
        return np.exp2(np.random.permutation(np.resize(levels, k // 32))).repeat(32)
    a = np.empty((k // 512, 16))
    for p in range(k // 512):
        a[p, :8] = np.random.permutation(np.resize(levels, 8))
        for g in range(8):
            far = levels[np.abs(levels - a[p, g]) >= 10]
            a[p, g + 8] = far[np.random.randint(len(far))]
    return np.exp2(a.ravel()).repeat(32)


def f64(x):
    return np.asarray(x).astype(np.float64)


def striped(idx):
    return np.tile(idx.reshape(-1, 16).T, (8, 1)).astype(np.uint16)


def unstriped(offs):
    return offs[:16].T.reshape(-1).astype(np.int64)


E2M1 = np.array([0.0, 0.5, 1.0, 1.5, 2.0, 3.0, 4.0, 6.0, -0.0, -0.5, -1.0, -1.5, -2.0, -3.0, -4.0, -6.0])


def pack_weight(w, fmt):
    k, n = w.shape
    w = f64(np.asarray(w, np.float32).astype(ml_dtypes.bfloat16)).reshape(k // 32, 32, n)
    amax = np.abs(w).max(1)
    if fmt == "e4m3":
        byte = np.frexp(amax)[1] - 1 + 127 - 7
    else:
        mant, ex = np.frexp(amax / 6.0)
        byte = np.where(mant > 0.5, ex, ex - 1) + 127
    byte = np.clip(np.where(amax > 0, byte, 1), 1, 254)
    scaled = (w * np.exp2(127.0 - byte)[:, None, :]).reshape(k, n).astype(np.float32)
    by_word = np.ascontiguousarray(scaled.reshape(k // 512, 128, 4, n).transpose(0, 1, 3, 2))
    if fmt == "e4m3":
        words = by_word.astype(ml_dtypes.float8_e4m3fn).view(np.uint8)
    else:
        c = by_word.astype(ml_dtypes.float4_e2m1fn).view(np.uint8) & 0xF
        words = (c[..., 0::2] | (c[..., 1::2] << 4)).reshape(k // 512, 128, 2 * n)
    return np.ascontiguousarray(words), np.ascontiguousarray(byte.astype(np.uint8).reshape(k // 512, 16, n))


def unpack_weight(words, scales, fmt):
    g, _, n = scales.shape
    words = np.ascontiguousarray(words).reshape(g, 128, n, -1)
    if fmt == "e4m3":
        vals = words.view(ml_dtypes.float8_e4m3fn).astype(np.float64)
    else:
        nib = np.empty((g, 128, n, 4), np.uint8)
        nib[..., 0::2] = words & 0xF
        nib[..., 1::2] = words >> 4
        vals = E2M1[nib]
    vals = vals * np.repeat(np.exp2(scales.astype(np.float64) - 127.0), 8, axis=1)[..., None]
    return vals.transpose(0, 1, 3, 2).reshape(g * 512, n)


def gelu(v):
    return 0.5 * v * (1.0 + np.tanh(np.sqrt(2.0 / np.pi) * (v + 0.044715 * v**3)))


K, M, H, N, T, S, T2, P, TL = 1024, 512, 512, 384, 2048, 1024, 2048, 512, 128

def setup_inputs():
    n = np.random.standard_normal
    s = mx_kscale(K)[:, None]
    s2 = mx_kscale(M)[:, None]
    u = mx_kscale(H)[:, None]
    tab_words, tab_scales = pack_weight(n((K, T)) * s, "e4m3")
    w3_words, w3_scales = pack_weight(n((K, H)) / np.sqrt(K) / s, "e2m1")
    perm = np.random.permutation(T2)
    return {
        "tab_words": tab_words, "tab_scales": tab_scales,
        "offs": striped(np.random.permutation(T)[:S]),
        "offs2": striped(np.random.permutation(T2)[:S]),
        "offs3": striped(perm[:P]),
        "offs4": striped(perm[P:2 * P]),
        "w1": (0.8 * n((K, H)) / np.sqrt(K) / s).astype(np.float32),
        "w2": (0.8 * n((M, H)) / np.sqrt(M) / s2).astype(np.float32),
        "canal": (n((M, S)) * s2).astype(np.float32),
        "w3_words": w3_words, "w3_scales": w3_scales,
        "gain": (np.exp(0.3 * n(H)) * u[:, 0]).astype(np.float32),
        "wgs": np.exp(0.3 * n((TL, S))).astype(np.float32),
        "page0": (n((H, T2)) * u).astype(np.float32),
        "ask": (0.6 * n(H) * u[:, 0]).astype(np.float32),
        "w4": (1.1 * n((H, N)) / np.sqrt(H) / u).astype(np.float32),
        "outw": np.exp(0.3 * n(N)).astype(np.float32),
    }

def reference(tab_words, tab_scales, offs, offs2, offs3, offs4, w1, w2, canal, w3_words, w3_scales, gain, wgs, page0, ask, w4, outw):
    v = unpack_weight(tab_words, tab_scales, "e4m3")[:, unstriped(offs)]
    y1 = mxq(f64(w1), 0, "e4m3").T @ v + mxq(f64(w2), 0, "e4m3").T @ mxq(f64(canal), 0, "e4m3")
    y2 = unpack_weight(w3_words, w3_scales, "e2m1").T @ v
    h = f64(gain)[:, None] * np.maximum(y1, y2)
    page = f64(page0).copy()
    page[:, unstriped(offs2)] = np.tile(f64(wgs), (H // TL, 1)) * h
    a = page[:, unstriped(offs3)]
    b = page[:, unstriped(offs4)]
    page[:, unstriped(offs3)] = np.minimum(a + f64(ask)[:, None], b)
    page[:, unstriped(offs4)] = a + b
    e = mxq(f64(w4), 0, "e4m3").T @ mxq(page, 0, "e4m3")
    return f64(outw)[:, None] * np.tanh(e)

@@ -1,0 +1,290 @@
+from contextlib import ExitStack
+
+import concourse.mybir as mybir
+
+K, M, H, N, T, S, PAIRS = 1024, 512, 512, 384, 2048, 1024, 512
+FLOPS = 2 * (K * H * S + M * H * S + K * H * S + H * N * T)
+
+F32 = mybir.dt.float32
+BF16 = mybir.dt.bfloat16
+I32 = mybir.dt.int32
+U32 = mybir.dt.uint32
+U16 = mybir.dt.uint16
+U8 = mybir.dt.uint8
+FP8X4 = mybir.dt.float8_e4m3fn_x4
+FP4X4 = mybir.dt.float4_e2m1fn_x4
+ALU = mybir.AluOpType
+ACT = mybir.ActivationFunctionType
+
+P = 128
+PACK = 4
+HALF = 512
+N_TILES = N // P
+PAGE_CHUNKS = (256, 256, 512, 512, 512)
+FIRST_PIECES = (256, 256, 512)
+
+
+def starts(widths):
+    return [sum(widths[:c]) for c in range(len(widths))]
+
+
+def tile_list_water_rights_exchange_kernel(
+    tc, tab_words, tab_scales, offs, offs2, offs3, offs4, w1, w2, canal, w3_words, w3_scales,
+    gain, wgs, page0, ask, w4, outw, out,
+):
+    nc = tc.nc
+    with ExitStack() as ctx:
+        lists = ctx.enter_context(tc.tile_pool(name="lists", bufs=1))
+        keep = ctx.enter_context(tc.tile_pool(name="keep", bufs=1))
+        shared = ctx.enter_context(tc.tile_pool(name="shared", bufs=1))
+        ring = ctx.enter_context(tc.tile_pool(name="ring", bufs=2))
+        psum = ctx.enter_context(tc.psum_pool(name="psum", bufs=4))
+
+        def held(shape, dtype, name):
+            return keep.tile(shape, dtype, name=name, align_bytes=64)
+
+        pick = lists.tile([P, S // 16], U16, name="pick")
+        put = lists.tile([P, S // 16], U16, name="put")
+        sellers = lists.tile([P, PAIRS // 16], U16, name="sellers")
+        buyers = lists.tile([P, PAIRS // 16], U16, name="buyers")
+
+        tab_w = [held([P, T], U32, f"tab_w{a}") for a in range(2)]
+        tab_s = held([P, T], U8, "tab_s")
+        w3_s_raw = held([P, 2, H], U8, "w3_s_raw")
+        v_s1 = held([P, S], U8, "v_s1")
+        nc.gpsimd.memset(tab_s[:].bitcast(I32), 0)
+        nc.gpsimd.memset(w3_s_raw[:].rearrange("p a c -> p (a c)").bitcast(I32), 0)
+        nc.gpsimd.memset(v_s1[:].bitcast(I32), 0)
+        gain_t = held([P, PACK], F32, "gain_t")
+        ask_t = held([P, PACK], F32, "ask_t")
+        outw_t = held([P, N_TILES], F32, "outw_t")
+
+        w1_raw = [held([P, PACK, H], F32, f"w1_raw{a}") for a in range(2)]
+        w2_raw = held([P, PACK, H], F32, "w2_raw")
+        w3_w_raw = held([P, 2, 2 * H], U8, "w3_w_raw")
+        canal_raw = [held([P, PACK, w], F32, f"canal_raw{c}") for c, w in enumerate(FIRST_PIECES)]
+        wgs_dealt = shared.tile([P, PACK, S], F32, name="wgs_dealt", offset=0, align_bytes=64)
+        page = [held([P, T], F32, f"page{t}") for t in range(PACK)]
+        w4_raw = held([P, PACK, N], F32, "w4_raw")
+
+        canal_rows = canal.rearrange("(p i) j -> p i j", i=PACK)
+        page_rows = page0.rearrange("(p t) c -> p t c", t=PACK)
+        wgs_rows = wgs.rearrange("(b t) j -> b t j", t=PACK)
+        piece_start = starts(FIRST_PIECES)
+
+        def load_words(a):
+            nc.sync.dma_start(out=tab_w[a][:].bitcast(I32),
+                              in_=tab_words[a].rearrange("p t i -> p (t i)").bitcast(I32))
+
+        def load_w1(a):
+            nc.sync.dma_start(out=w1_raw[a][:],
+                              in_=w1[512 * a:512 * (a + 1), :].rearrange("(p i) c -> p i c", i=PACK))
+
+        def load_canal(c):
+            nc.sync.dma_start(out=canal_raw[c][:],
+                              in_=canal_rows[:, :, piece_start[c]:piece_start[c] + FIRST_PIECES[c]])
+
+        nc.sync.dma_start(pick[:], offs)
+        load_words(0)
+        for q in range(4):
+            nc.sync.dma_start(out=tab_s[32 * q:32 * q + 8, :].bitcast(I32),
+                              in_=tab_scales[:, 4 * q:4 * q + 4, :].bitcast(I32))
+        load_w1(0)
+        load_words(1)
+        nc.sync.dma_start(out=w3_w_raw[:].bitcast(I32), in_=w3_words.rearrange("a p c -> p a c").bitcast(I32))
+        for q in range(4):
+            nc.sync.dma_start(out=w3_s_raw[32 * q:32 * q + 4, :, :].bitcast(I32),
+                              in_=w3_scales[:, 4 * q:4 * q + 4, :].rearrange("a r c -> r a c").bitcast(I32))
+        load_w1(1)
+        nc.sync.dma_start(out=w2_raw[:], in_=w2.rearrange("(p i) c -> p i c", i=PACK))
+
+        v_w = [[held([P, HALF], U32, f"v_w{a}_{h}") for h in range(2)] for a in range(2)]
+        v_s = held([P, S], U8, "v_s")
+
+        def gather_words(a, h):
+            nc.vector.tensor_copy(v_w[a][h][:], tab_w[a][:].indirect(pick[:, 32 * h:32 * (h + 1)]))
+
+        gather_words(0, 0)
+        nc.vector.tensor_copy(v_s[:], tab_s[:].indirect(pick[:]))
+        for q in range(4):
+            nc.sync.dma_start(out=v_s1[32 * q:32 * q + 4, :].bitcast(I32),
+                              in_=v_s[32 * q + 4:32 * q + 8, :].bitcast(I32))
+        gather_words(1, 0)
+        v_planes = [v_s, v_s1]
+
+        nc.sync.dma_start(put[:], offs2)
+        nc.sync.dma_start(out=gain_t[:], in_=gain.rearrange("(p t) -> p t", t=PACK))
+        load_canal(0)
+        for q in range(4):
+            nc.sync.dma_start(out=wgs_dealt[32 * q:32 * (q + 1), 0, :], in_=wgs_rows[:, 0, :])
+        nc.sync.dma_start(out=page[0][:], in_=page_rows[:, 0, :])
+        load_canal(1)
+        load_canal(2)
+        nc.sync.dma_start(sellers[:], offs3)
+        nc.sync.dma_start(buyers[:], offs4)
+        for q in range(4):
+            nc.sync.dma_start(out=wgs_dealt[32 * q:32 * (q + 1), 1:PACK, :], in_=wgs_rows[:, 1:PACK, :])
+        nc.sync.dma_start(out=ask_t[:], in_=ask.rearrange("(p t) -> p t", t=PACK))
+        nc.sync.dma_start(out=w4_raw[:], in_=w4.rearrange("(p i) n -> p i n", i=PACK))
+        for t in range(1, PACK):
+            nc.sync.dma_start(out=page[t][:], in_=page_rows[:, t, :])
+        nc.sync.dma_start(out=outw_t[:], in_=outw.rearrange("(p c) -> p c", c=N_TILES))
+
+        w3_w = held([P, 2, 2 * H], U8, "w3_w")
+        w3_s = held([P, 2, H], U8, "w3_s")
+        nc.vector.tensor_copy(out=w3_w[:].bitcast(U16).rearrange("p a (t m) -> p a t m", t=PACK),
+                              in_=w3_w_raw[:].bitcast(U16).rearrange("p a (m t) -> p a t m", t=PACK))
+        nc.vector.tensor_copy(out=w3_s[:].rearrange("p a (t m) -> p a t m", t=PACK),
+                              in_=w3_s_raw[:].rearrange("p a (m t) -> p a t m", t=PACK))
+
+        def quantise(grouped, width, name):
+            codes = held([P, width], U32, name + "_codes")
+            scales = held([P, width], U8, name + "_scales")
+            nc.vector.quantize_mx(out=codes[:].bitcast(FP8X4), scales=scales[:], in_=grouped[:])
+            return codes, scales
+
+        def round_weight(copy, raw, groups, name):
+            width = raw.shape[2]
+            grouped = held([P, width * PACK], BF16, name + "_bf16")
+            copy(out=grouped[:].rearrange("p (t m i) -> p m i t", t=groups, i=PACK),
+                 in_=raw[:].rearrange("p i (m t) -> p m i t", t=groups))
+            return grouped
+
+        def round_rows(copy, raw, name):
+            width = raw.shape[2]
+            grouped = held([P, width * PACK], BF16, name + "_bf16")
+            copy(out=grouped[:].rearrange("p (c e i) -> p c i e", e=4, i=PACK),
+                 in_=raw[:].rearrange("p i (c e) -> p c i e", e=4))
+            return grouped
+
+        w1_b = [round_weight(nc.scalar.copy, w1_raw[a], PACK, f"w1_{a}") for a in range(2)]
+        w1_q = [quantise(w1_b[0], H, "w1_0")]
+        w2_b = round_weight(nc.vector.tensor_copy, w2_raw, PACK, "w2")
+        w1_q.append(quantise(w1_b[1], H, "w1_1"))
+        canal_b = [round_rows(nc.vector.tensor_copy, canal_raw[0], "canal0")]
+        w2_q = quantise(w2_b, H, "w2")
+        canal_q = [quantise(canal_b[0], FIRST_PIECES[0], "canal0")]
+
+        y2 = [[held([P, HALF], F32, f"y2_{t}_{h}") for h in range(2)] for t in range(PACK)]
+        weight = [held([P, S], F32, f"weight{t}") for t in range(PACK)]
+
+        def second_reading(t, h):
+            acc = psum.tile([P, HALF], F32, name="acc_late")
+            for a in range(2):
+                nc.tensor.matmul_mx(
+                    out=acc[:], lhsT=w3_w[:, a, 2 * P * t:2 * P * (t + 1)].bitcast(FP4X4),
+                    lhsT_scale=w3_s[:, a, P * t:P * (t + 1)],
+                    rhs=v_w[a][h][:].bitcast(FP8X4), rhs_scale=v_planes[a][:, HALF * h:HALF * (h + 1)],
+                    start=(a == 0), stop=(a == 1))
+            nc.scalar.copy(out=y2[t][h][:], in_=acc[:])
+
+        def first_reading(acc, t, c):
+            j0, width = piece_start[c], FIRST_PIECES[c]
+            h, lo = divmod(j0, HALF)
+            rows = slice(P * t, P * (t + 1))
+            for a in range(2):
+                nc.tensor.matmul_mx(
+                    out=acc, lhsT=w1_q[a][0][:, rows].bitcast(FP8X4), lhsT_scale=w1_q[a][1][:, rows],
+                    rhs=v_w[a][h][:, lo:lo + width].bitcast(FP8X4), rhs_scale=v_planes[a][:, j0:j0 + width],
+                    start=(a == 0), stop=False)
+            nc.tensor.matmul_mx(
+                out=acc, lhsT=w2_q[0][:, rows].bitcast(FP8X4), lhsT_scale=w2_q[1][:, rows],
+                rhs=canal_q[c][0][:].bitcast(FP8X4), rhs_scale=canal_q[c][1][:], start=False, stop=True)
+
+        def larger(t, pieces):
+            j0 = piece_start[pieces[0]]
+            width = sum(FIRST_PIECES[c] for c in pieces)
+            h, lo = divmod(j0, HALF)
+            acc = psum.tile([P, width], F32, name="acc_y1")
+            for c in pieces:
+                first_reading(acc[:, piece_start[c] - j0:piece_start[c] - j0 + FIRST_PIECES[c]], t, c)
+            top = ring.tile([P, width], F32, name="top")
+            nc.vector.tensor_tensor(out=top[:], in0=acc[:], in1=y2[t][h][:, lo:lo + width], op=ALU.max)
+            return top, j0, width
+
+        def place(t, made):
+            top, j0, width = made
+            nc.vector.tensor_tensor(page[t][:].indirect(put[:, j0 // 16:(j0 + width) // 16]),
+                                    top[:], weight[t][:, j0:j0 + width], ALU.mult)
+
+        second_reading(0, 0)
+        nc.scalar.activation(out=weight[0][:], in_=wgs_dealt[:, 0, :], func=ACT.Copy, scale=gain_t[:, 0:1])
+        place(0, larger(0, [0]))
+        canal_b.append(round_rows(nc.scalar.copy, canal_raw[1], "canal1"))
+        canal_b.append(round_rows(nc.scalar.copy, canal_raw[2], "canal2"))
+        gather_words(0, 1)
+        gather_words(1, 1)
+        second_reading(0, 1)
+        canal_q.append(quantise(canal_b[1], FIRST_PIECES[1], "canal1"))
+        place(0, larger(0, [1]))
+        canal_q.append(quantise(canal_b[2], FIRST_PIECES[2], "canal2"))
+        place(0, larger(0, [2]))
+        for t in range(1, PACK):
+            for h in range(2):
+                second_reading(t, h)
+            nc.scalar.activation(out=weight[t][:], in_=wgs_dealt[:, t, :], func=ACT.Copy,
+                                 scale=gain_t[:, t:t + 1])
+        w4_b = round_weight(nc.scalar.copy, w4_raw, N_TILES, "w4")
+        w4_q = quantise(w4_b, N, "w4")
+
+        chunk_start = starts(PAGE_CHUNKS)
+        woven = [shared.tile([P, w, PACK], BF16, name=f"woven{c}", offset=2 * PACK * chunk_start[c], align_bytes=64)
+                 for c, w in enumerate(PAGE_CHUNKS)]
+
+        def weave(copy, t, c):
+            copy(out=woven[c][:, :, t], in_=page[t][:, chunk_start[c]:chunk_start[c] + PAGE_CHUNKS[c]])
+
+        for t in range(PACK):
+            last = t == PACK - 1
+            sell = ring.tile([P, PAIRS], F32, name="sell")
+            buy = ring.tile([P, PAIRS], F32, name="buy")
+            nc.vector.tensor_copy(sell[:], page[t][:].indirect(sellers[:]))
+            nc.vector.tensor_copy(buy[:], page[t][:].indirect(buyers[:]))
+            if not last:
+                early = larger(t + 1, [0, 1])
+            nc.vector.tensor_tensor(page[t][:].indirect(buyers[:]), sell[:], buy[:], ALU.add)
+            if last:
+                low = keep.tile([P, PAIRS], F32, name="low_last", tag=f"page{t - 1}", align_bytes=64)
+            else:
+                low = ring.tile([P, PAIRS], F32, name="low")
+            nc.vector.scalar_tensor_tensor(out=low[:], in0=sell[:], scalar=ask_t[:, t:t + 1], in1=buy[:],
+                                           op0=ALU.add, op1=ALU.min)
+            if not last:
+                late = larger(t + 1, [2])
+                place(t + 1, early)
+            nc.vector.tensor_copy(page[t][:].indirect(sellers[:]), low[:])
+            if not last:
+                place(t + 1, late)
+                for c in range(len(PAGE_CHUNKS)):
+                    weave(nc.scalar.copy, t, c)
+
+        out_rows = out.rearrange("(p c) t -> p c t", c=N_TILES)
+
+        def score(c, quantised):
+            cols = slice(chunk_start[c], chunk_start[c] + PAGE_CHUNKS[c])
+            for n in range(N_TILES):
+                acc = psum.tile([P, PAGE_CHUNKS[c]], F32, name="acc_late")
+                nc.tensor.matmul_mx(
+                    out=acc[:], lhsT=w4_q[0][:, P * n:P * (n + 1)].bitcast(FP8X4),
+                    lhsT_scale=w4_q[1][:, P * n:P * (n + 1)],
+                    rhs=quantised[0][:].bitcast(FP8X4), rhs_scale=quantised[1][:], start=True, stop=True)
+                bent = ring.tile([P, PAGE_CHUNKS[c]], F32, name="bent", bufs=6)
+                nc.scalar.activation(out=bent[:], in_=acc[:], func=ACT.Tanh)
+                nc.vector.tensor_scalar(out=bent[:], in0=bent[:], scalar1=outw_t[:, n:n + 1], scalar2=None,
+                                        op0=ALU.mult)
+                nc.sync.dma_start(out=out_rows[:, n, cols], in_=bent[:])
+
+        chunks = len(PAGE_CHUNKS)
+        weave(nc.vector.tensor_copy, PACK - 1, 0)
+        waiting = None
+        for c in range(chunks):
+            if c + 1 < chunks:
+                weave(nc.vector.tensor_copy, PACK - 1, c + 1)
+            codes = held([P, PAGE_CHUNKS[c]], U32, f"page_codes{c}")
+            scales = held([P, PAGE_CHUNKS[c]], U8, f"page_scales{c}")
+            nc.vector.quantize_mx(out=codes[:].bitcast(FP8X4), scales=scales[:],
+                                  in_=woven[c][:].rearrange("p c i -> p (c i)"))
+            if waiting is not None:
+                score(c - 1, waiting)
+            waiting = (codes, scales)
+        score(chunks - 1, waiting)

@@ -18,14 +18,15 @@ ACT = mybir.ActivationFunctionType
 
 P = 128
 PACK = 4
+QUADRANTS = 4
+PER_COLUMN = 16
+PASS = P * PACK
 HALF = 512
+PIECE = 256
 N_TILES = N // P
-PAGE_CHUNKS = (256, 256, 512, 512, 512)
-FIRST_PIECES = (256, 256, 512)
-
-
-def starts(widths):
-    return [sum(widths[:c]) for c in range(len(widths))]
+LAST = PACK - 1
+PAGE_CHUNKS = (256, 512, 256, 512, 256, 256)
+SCALAR_TAIL_CHUNKS = 2
 
 
 def tile_list_water_rights_exchange_kernel(
@@ -40,13 +41,13 @@ def tile_list_water_rights_exchange_kernel(
         ring = ctx.enter_context(tc.tile_pool(name="ring", bufs=2))
         psum = ctx.enter_context(tc.psum_pool(name="psum", bufs=4))
 
-        def held(shape, dtype, name):
-            return keep.tile(shape, dtype, name=name, align_bytes=64)
+        def held(shape, dtype, name, tag=""):
+            return keep.tile(shape, dtype, name=name, tag=tag or name, align_bytes=64)
 
-        pick = lists.tile([P, S // 16], U16, name="pick")
-        put = lists.tile([P, S // 16], U16, name="put")
-        sellers = lists.tile([P, PAIRS // 16], U16, name="sellers")
-        buyers = lists.tile([P, PAIRS // 16], U16, name="buyers")
+        pick = lists.tile([P, S // PER_COLUMN], U16, name="pick")
+        put = lists.tile([P, S // PER_COLUMN], U16, name="put")
+        sellers = lists.tile([P, PAIRS // PER_COLUMN], U16, name="sellers")
+        buyers = lists.tile([P, PAIRS // PER_COLUMN], U16, name="buyers")
 
         tab_w = [held([P, T], U32, f"tab_w{a}") for a in range(2)]
         tab_s = held([P, T], U8, "tab_s")
@@ -62,7 +63,7 @@ def tile_list_water_rights_exchange_kernel(
         w1_raw = [held([P, PACK, H], F32, f"w1_raw{a}") for a in range(2)]
         w2_raw = held([P, PACK, H], F32, "w2_raw")
         w3_w_raw = held([P, 2, 2 * H], U8, "w3_w_raw")
-        canal_raw = [held([P, PACK, w], F32, f"canal_raw{c}") for c, w in enumerate(FIRST_PIECES)]
+        canal_raw = [held([P, PACK, PIECE], F32, f"canal_raw{c}") for c in range(S // PIECE)]
         wgs_dealt = shared.tile([P, PACK, S], F32, name="wgs_dealt", offset=0, align_bytes=64)
         page = [held([P, T], F32, f"page{t}") for t in range(PACK)]
         w4_raw = held([P, PACK, N], F32, "w4_raw")
@@ -70,7 +71,6 @@ def tile_list_water_rights_exchange_kernel(
         canal_rows = canal.rearrange("(p i) j -> p i j", i=PACK)
         page_rows = page0.rearrange("(p t) c -> p t c", t=PACK)
         wgs_rows = wgs.rearrange("(b t) j -> b t j", t=PACK)
-        piece_start = starts(FIRST_PIECES)
 
         def load_words(a):
             nc.sync.dma_start(out=tab_w[a][:].bitcast(I32),
@@ -78,213 +78,237 @@ def tile_list_water_rights_exchange_kernel(
 
         def load_w1(a):
             nc.sync.dma_start(out=w1_raw[a][:],
-                              in_=w1[512 * a:512 * (a + 1), :].rearrange("(p i) c -> p i c", i=PACK))
+                              in_=w1[PASS * a:PASS * (a + 1), :].rearrange("(p i) c -> p i c", i=PACK))
 
-        def load_canal(c):
-            nc.sync.dma_start(out=canal_raw[c][:],
-                              in_=canal_rows[:, :, piece_start[c]:piece_start[c] + FIRST_PIECES[c]])
+        def load_wgs(first, end):
+            for q in range(QUADRANTS):
+                nc.sync.dma_start(out=wgs_dealt[32 * q:32 * (q + 1), first:end, :], in_=wgs_rows[:, first:end, :])
 
-        nc.sync.dma_start(pick[:], offs)
-        load_words(0)
-        for q in range(4):
-            nc.sync.dma_start(out=tab_s[32 * q:32 * q + 8, :].bitcast(I32),
-                              in_=tab_scales[:, 4 * q:4 * q + 4, :].bitcast(I32))
-        load_w1(0)
-        load_words(1)
-        nc.sync.dma_start(out=w3_w_raw[:].bitcast(I32), in_=w3_words.rearrange("a p c -> p a c").bitcast(I32))
-        for q in range(4):
-            nc.sync.dma_start(out=w3_s_raw[32 * q:32 * q + 4, :, :].bitcast(I32),
-                              in_=w3_scales[:, 4 * q:4 * q + 4, :].rearrange("a r c -> r a c").bitcast(I32))
-        load_w1(1)
-        nc.sync.dma_start(out=w2_raw[:], in_=w2.rearrange("(p i) c -> p i c", i=PACK))
+        def load_page(t):
+            nc.sync.dma_start(out=page[t][:], in_=page_rows[:, t, :])
 
         v_w = [[held([P, HALF], U32, f"v_w{a}_{h}") for h in range(2)] for a in range(2)]
         v_s = held([P, S], U8, "v_s")
-
-        def gather_words(a, h):
-            nc.vector.tensor_copy(v_w[a][h][:], tab_w[a][:].indirect(pick[:, 32 * h:32 * (h + 1)]))
-
-        gather_words(0, 0)
-        nc.vector.tensor_copy(v_s[:], tab_s[:].indirect(pick[:]))
-        for q in range(4):
-            nc.sync.dma_start(out=v_s1[32 * q:32 * q + 4, :].bitcast(I32),
-                              in_=v_s[32 * q + 4:32 * q + 8, :].bitcast(I32))
-        gather_words(1, 0)
         v_planes = [v_s, v_s1]
 
-        nc.sync.dma_start(put[:], offs2)
-        nc.sync.dma_start(out=gain_t[:], in_=gain.rearrange("(p t) -> p t", t=PACK))
-        load_canal(0)
-        for q in range(4):
-            nc.sync.dma_start(out=wgs_dealt[32 * q:32 * (q + 1), 0, :], in_=wgs_rows[:, 0, :])
-        nc.sync.dma_start(out=page[0][:], in_=page_rows[:, 0, :])
-        load_canal(1)
-        load_canal(2)
-        nc.sync.dma_start(sellers[:], offs3)
-        nc.sync.dma_start(buyers[:], offs4)
-        for q in range(4):
-            nc.sync.dma_start(out=wgs_dealt[32 * q:32 * (q + 1), 1:PACK, :], in_=wgs_rows[:, 1:PACK, :])
-        nc.sync.dma_start(out=ask_t[:], in_=ask.rearrange("(p t) -> p t", t=PACK))
-        nc.sync.dma_start(out=w4_raw[:], in_=w4.rearrange("(p i) n -> p i n", i=PACK))
-        for t in range(1, PACK):
-            nc.sync.dma_start(out=page[t][:], in_=page_rows[:, t, :])
-        nc.sync.dma_start(out=outw_t[:], in_=outw.rearrange("(p c) -> p c", c=N_TILES))
+        def entries(offsets, first, end):
+            return offsets[:, first // PER_COLUMN:end // PER_COLUMN]
 
+        def gather_words(a, h):
+            nc.vector.tensor_copy(v_w[a][h][:], tab_w[a][:].indirect(entries(pick, HALF * h, HALF * (h + 1))))
+
+        nc.sync.dma_start(pick[:], offs)
+        nc.sync.dma_start(out=w3_w_raw[:].bitcast(I32), in_=w3_words.rearrange("a p c -> p a c").bitcast(I32))
+        for q in range(QUADRANTS):
+            nc.sync.dma_start(out=tab_s[32 * q:32 * q + 8, :].bitcast(I32),
+                              in_=tab_scales[:, 4 * q:4 * q + 4, :].bitcast(I32))
+        load_words(0)
+        load_words(1)
+        load_w1(0)
+        for q in range(QUADRANTS):
+            nc.sync.dma_start(out=w3_s_raw[32 * q:32 * q + 4, :, :].bitcast(I32),
+                              in_=w3_scales[:, 4 * q:4 * q + 4, :].rearrange("a e c -> e a c").bitcast(I32))
+        load_w1(1)
         w3_w = held([P, 2, 2 * H], U8, "w3_w")
         w3_s = held([P, 2, H], U8, "w3_s")
-        nc.vector.tensor_copy(out=w3_w[:].bitcast(U16).rearrange("p a (t m) -> p a t m", t=PACK),
-                              in_=w3_w_raw[:].bitcast(U16).rearrange("p a (m t) -> p a t m", t=PACK))
-        nc.vector.tensor_copy(out=w3_s[:].rearrange("p a (t m) -> p a t m", t=PACK),
+        nc.vector.tensor_copy(out=w3_w[:].bitcast(U16).rearrange("p a (t m) -> p a m t", t=PACK),
+                              in_=w3_w_raw[:].bitcast(U16).rearrange("p a (m t) -> p a m t", t=PACK))
+        nc.vector.tensor_copy(v_s[:], tab_s[:].indirect(pick[:]))
+        for q in range(QUADRANTS):
+            nc.sync.dma_start(out=v_s1[32 * q:32 * q + 4, :].bitcast(I32),
+                              in_=v_s[32 * q + 4:32 * q + 8, :].bitcast(I32))
+        nc.sync.dma_start(out=w2_raw[:], in_=w2.rearrange("(p i) c -> p i c", i=PACK))
+        gather_words(0, 0)
+        nc.sync.dma_start(put[:], offs2)
+        nc.sync.dma_start(out=gain_t[:], in_=gain.rearrange("(p t) -> p t", t=PACK))
+        for c in range(S // PIECE):
+            nc.sync.dma_start(out=canal_raw[c][:], in_=canal_rows[:, :, PIECE * c:PIECE * (c + 1)])
+        load_wgs(0, 1)
+        load_page(0)
+        load_wgs(1, 2)
+        load_page(1)
+        nc.sync.dma_start(sellers[:], offs3)
+        nc.sync.dma_start(buyers[:], offs4)
+        nc.sync.dma_start(out=ask_t[:], in_=ask.rearrange("(p t) -> p t", t=PACK))
+        load_wgs(2, PACK)
+        nc.sync.dma_start(out=w4_raw[:], in_=w4.rearrange("(p i) n -> p i n", i=PACK))
+        load_page(2)
+        load_page(3)
+        nc.sync.dma_start(out=outw_t[:], in_=outw.rearrange("(p c) -> p c", c=N_TILES))
+
+        nc.gpsimd.tensor_copy(out=w3_s[:].rearrange("p a (t m) -> p a t m", t=PACK),
                               in_=w3_s_raw[:].rearrange("p a (m t) -> p a t m", t=PACK))
+        gather_words(1, 0)
 
         def quantise(grouped, width, name):
             codes = held([P, width], U32, name + "_codes")
             scales = held([P, width], U8, name + "_scales")
-            nc.vector.quantize_mx(out=codes[:].bitcast(FP8X4), scales=scales[:], in_=grouped[:])
+            nc.vector.quantize_mx(out=codes[:].bitcast(FP8X4), scales=scales[:], in_=grouped)
             return codes, scales
 
         def round_weight(copy, raw, groups, name):
-            width = raw.shape[2]
-            grouped = held([P, width * PACK], BF16, name + "_bf16")
+            grouped = held([P, raw.shape[2] * PACK], BF16, name + "_bf16")
             copy(out=grouped[:].rearrange("p (t m i) -> p m i t", t=groups, i=PACK),
                  in_=raw[:].rearrange("p i (m t) -> p m i t", t=groups))
-            return grouped
+            return grouped[:]
 
-        def round_rows(copy, raw, name):
-            width = raw.shape[2]
-            grouped = held([P, width * PACK], BF16, name + "_bf16")
+        def round_canal(copy, c):
+            grouped = held([P, PIECE * PACK], BF16, f"canal{c}_bf16")
             copy(out=grouped[:].rearrange("p (c e i) -> p c i e", e=4, i=PACK),
-                 in_=raw[:].rearrange("p i (c e) -> p c i e", e=4))
-            return grouped
+                 in_=canal_raw[c][:].rearrange("p i (c e) -> p c i e", e=4))
+            return grouped[:]
 
         w1_b = [round_weight(nc.scalar.copy, w1_raw[a], PACK, f"w1_{a}") for a in range(2)]
         w1_q = [quantise(w1_b[0], H, "w1_0")]
         w2_b = round_weight(nc.vector.tensor_copy, w2_raw, PACK, "w2")
         w1_q.append(quantise(w1_b[1], H, "w1_1"))
-        canal_b = [round_rows(nc.vector.tensor_copy, canal_raw[0], "canal0")]
+        canal_b = [round_canal(nc.vector.tensor_copy, 0)]
         w2_q = quantise(w2_b, H, "w2")
-        canal_q = [quantise(canal_b[0], FIRST_PIECES[0], "canal0")]
+        canal_q = [quantise(canal_b[0], PIECE, "canal0")]
 
-        y2 = [[held([P, HALF], F32, f"y2_{t}_{h}") for h in range(2)] for t in range(PACK)]
+        top = [held([P, S], F32, f"top{t}") for t in range(PACK)]
         weight = [held([P, S], F32, f"weight{t}") for t in range(PACK)]
 
-        def second_reading(t, h):
-            acc = psum.tile([P, HALF], F32, name="acc_late")
+        def top_half(t, h):
+            return top[t][:, HALF * h:HALF * (h + 1)]
+
+        def second_sum(t, h):
+            acc = psum.tile([P, HALF], F32, name="acc_scalar")
             for a in range(2):
                 nc.tensor.matmul_mx(
                     out=acc[:], lhsT=w3_w[:, a, 2 * P * t:2 * P * (t + 1)].bitcast(FP4X4),
                     lhsT_scale=w3_s[:, a, P * t:P * (t + 1)],
                     rhs=v_w[a][h][:].bitcast(FP8X4), rhs_scale=v_planes[a][:, HALF * h:HALF * (h + 1)],
                     start=(a == 0), stop=(a == 1))
-            nc.scalar.copy(out=y2[t][h][:], in_=acc[:])
+            nc.scalar.copy(out=top_half(t, h), in_=acc[:])
 
-        def first_reading(acc, t, c):
-            j0, width = piece_start[c], FIRST_PIECES[c]
-            h, lo = divmod(j0, HALF)
+        def larger(t, h, into):
+            acc = psum.tile([P, HALF], F32, name="acc_first")
             rows = slice(P * t, P * (t + 1))
-            for a in range(2):
+            for e in range(HALF // PIECE):
+                cols = slice(PIECE * e, PIECE * (e + 1))
+                c = (HALF // PIECE) * h + e
+                for a in range(2):
+                    nc.tensor.matmul_mx(
+                        out=acc[:, cols], lhsT=w1_q[a][0][:, rows].bitcast(FP8X4), lhsT_scale=w1_q[a][1][:, rows],
+                        rhs=v_w[a][h][:, cols].bitcast(FP8X4), rhs_scale=v_planes[a][:, PIECE * c:PIECE * (c + 1)],
+                        start=(a == 0), stop=False)
                 nc.tensor.matmul_mx(
-                    out=acc, lhsT=w1_q[a][0][:, rows].bitcast(FP8X4), lhsT_scale=w1_q[a][1][:, rows],
-                    rhs=v_w[a][h][:, lo:lo + width].bitcast(FP8X4), rhs_scale=v_planes[a][:, j0:j0 + width],
-                    start=(a == 0), stop=False)
-            nc.tensor.matmul_mx(
-                out=acc, lhsT=w2_q[0][:, rows].bitcast(FP8X4), lhsT_scale=w2_q[1][:, rows],
-                rhs=canal_q[c][0][:].bitcast(FP8X4), rhs_scale=canal_q[c][1][:], start=False, stop=True)
+                    out=acc[:, cols], lhsT=w2_q[0][:, rows].bitcast(FP8X4), lhsT_scale=w2_q[1][:, rows],
+                    rhs=canal_q[c][0][:].bitcast(FP8X4), rhs_scale=canal_q[c][1][:], start=False, stop=True)
+            nc.vector.tensor_tensor(out=into, in0=acc[:], in1=top_half(t, h), op=ALU.max)
 
-        def larger(t, pieces):
-            j0 = piece_start[pieces[0]]
-            width = sum(FIRST_PIECES[c] for c in pieces)
-            h, lo = divmod(j0, HALF)
-            acc = psum.tile([P, width], F32, name="acc_y1")
-            for c in pieces:
-                first_reading(acc[:, piece_start[c] - j0:piece_start[c] - j0 + FIRST_PIECES[c]], t, c)
-            top = ring.tile([P, width], F32, name="top")
-            nc.vector.tensor_tensor(out=top[:], in0=acc[:], in1=y2[t][h][:, lo:lo + width], op=ALU.max)
-            return top, j0, width
+        def place(t, h, values):
+            nc.vector.tensor_tensor(page[t][:].indirect(entries(put, HALF * h, HALF * (h + 1))),
+                                    values, weight[t][:, HALF * h:HALF * (h + 1)], ALU.mult)
 
-        def place(t, made):
-            top, j0, width = made
-            nc.vector.tensor_tensor(page[t][:].indirect(put[:, j0 // 16:(j0 + width) // 16]),
-                                    top[:], weight[t][:, j0:j0 + width], ALU.mult)
+        def weigh(t):
+            nc.scalar.activation(out=weight[t][:], in_=wgs_dealt[:, t, :], func=ACT.Copy, scale=gain_t[:, t:t + 1])
 
-        second_reading(0, 0)
-        nc.scalar.activation(out=weight[0][:], in_=wgs_dealt[:, 0, :], func=ACT.Copy, scale=gain_t[:, 0:1])
-        place(0, larger(0, [0]))
-        canal_b.append(round_rows(nc.scalar.copy, canal_raw[1], "canal1"))
-        canal_b.append(round_rows(nc.scalar.copy, canal_raw[2], "canal2"))
+        canal_b.append(round_canal(nc.vector.tensor_copy, 1))
         gather_words(0, 1)
         gather_words(1, 1)
-        second_reading(0, 1)
-        canal_q.append(quantise(canal_b[1], FIRST_PIECES[1], "canal1"))
-        place(0, larger(0, [1]))
-        canal_q.append(quantise(canal_b[2], FIRST_PIECES[2], "canal2"))
-        place(0, larger(0, [2]))
+        canal_q.append(quantise(canal_b[1], PIECE, "canal1"))
+        canal_b.append(round_canal(nc.scalar.copy, 2))
+        canal_b.append(round_canal(nc.scalar.copy, 3))
+        weigh(0)
+        for h in range(2):
+            for t in range(PACK):
+                second_sum(t, h)
+        larger(0, 0, top_half(0, 0))
+        canal_q.append(quantise(canal_b[2], PIECE, "canal2"))
+        larger(1, 0, top_half(1, 0))
+        canal_q.append(quantise(canal_b[3], PIECE, "canal3"))
+        larger(2, 0, top_half(2, 0))
+        larger(3, 0, top_half(3, 0))
+        place(0, 0, top_half(0, 0))
+        larger(0, 1, top_half(0, 1))
+        larger(1, 1, top_half(1, 1))
+        place(0, 1, top_half(0, 1))
+        larger(2, 1, top_half(2, 1))
         for t in range(1, PACK):
-            for h in range(2):
-                second_reading(t, h)
-            nc.scalar.activation(out=weight[t][:], in_=wgs_dealt[:, t, :], func=ACT.Copy,
-                                 scale=gain_t[:, t:t + 1])
+            weigh(t)
         w4_b = round_weight(nc.scalar.copy, w4_raw, N_TILES, "w4")
-        w4_q = quantise(w4_b, N, "w4")
 
-        chunk_start = starts(PAGE_CHUNKS)
+        chunk_start = [sum(PAGE_CHUNKS[:c]) for c in range(len(PAGE_CHUNKS))]
         woven = [shared.tile([P, w, PACK], BF16, name=f"woven{c}", offset=2 * PACK * chunk_start[c], align_bytes=64)
                  for c, w in enumerate(PAGE_CHUNKS)]
 
         def weave(copy, t, c):
             copy(out=woven[c][:, :, t], in_=page[t][:, chunk_start[c]:chunk_start[c] + PAGE_CHUNKS[c]])
 
-        for t in range(PACK):
-            last = t == PACK - 1
+        def fetch(t):
             sell = ring.tile([P, PAIRS], F32, name="sell")
             buy = ring.tile([P, PAIRS], F32, name="buy")
             nc.vector.tensor_copy(sell[:], page[t][:].indirect(sellers[:]))
             nc.vector.tensor_copy(buy[:], page[t][:].indirect(buyers[:]))
-            if not last:
-                early = larger(t + 1, [0, 1])
+            return sell, buy
+
+        def settle_buyers(t, pair, low):
+            sell, buy = pair
             nc.vector.tensor_tensor(page[t][:].indirect(buyers[:]), sell[:], buy[:], ALU.add)
-            if last:
-                low = keep.tile([P, PAIRS], F32, name="low_last", tag=f"page{t - 1}", align_bytes=64)
-            else:
-                low = ring.tile([P, PAIRS], F32, name="low")
             nc.vector.scalar_tensor_tensor(out=low[:], in0=sell[:], scalar=ask_t[:, t:t + 1], in1=buy[:],
                                            op0=ALU.add, op1=ALU.min)
-            if not last:
-                late = larger(t + 1, [2])
-                place(t + 1, early)
+
+        def settle_sellers(t, low):
             nc.vector.tensor_copy(page[t][:].indirect(sellers[:]), low[:])
-            if not last:
-                place(t + 1, late)
-                for c in range(len(PAGE_CHUNKS)):
-                    weave(nc.scalar.copy, t, c)
+
+        def weave_on_scalar(t):
+            for c in range(len(PAGE_CHUNKS)):
+                weave(nc.scalar.copy, t, c)
+
+        for t in range(LAST - 1):
+            pair = fetch(t)
+            place(t + 1, 0, top_half(t + 1, 0))
+            low = ring.tile([P, PAIRS], F32, name="low")
+            settle_buyers(t, pair, low)
+            place(t + 1, 1, top_half(t + 1, 1))
+            settle_sellers(t, low)
+            weave_on_scalar(t)
+        w4_q = quantise(w4_b, N, "w4")
+
+        pair = fetch(LAST - 1)
+        place(LAST, 0, top_half(LAST, 0))
+        low = held([P, PAIRS], F32, "low_before_last")
+        settle_buyers(LAST - 1, pair, low)
+        settle_sellers(LAST - 1, low)
+        weave_on_scalar(LAST - 1)
+        top_last = held([P, HALF], F32, "top_last", tag="low_before_last")
+        larger(LAST, 1, top_last[:])
+        place(LAST, 1, top_last[:])
+
+        pair = fetch(LAST)
+        low = held([P, PAIRS], F32, "low_last", tag=f"page{LAST - 1}")
+        settle_buyers(LAST, pair, low)
+        settle_sellers(LAST, low)
 
         out_rows = out.rearrange("(p c) t -> p c t", c=N_TILES)
+        spent = ("w1_raw0", "w1_raw1", "w2_raw", "page0", "page1", "w4_raw")
 
         def score(c, quantised):
             cols = slice(chunk_start[c], chunk_start[c] + PAGE_CHUNKS[c])
+            result = held([P, N_TILES, PAGE_CHUNKS[c]], F32, f"result{c}", tag=spent[c])
             for n in range(N_TILES):
-                acc = psum.tile([P, PAGE_CHUNKS[c]], F32, name="acc_late")
+                acc = psum.tile([P, PAGE_CHUNKS[c]], F32, name="acc_scalar")
                 nc.tensor.matmul_mx(
                     out=acc[:], lhsT=w4_q[0][:, P * n:P * (n + 1)].bitcast(FP8X4),
                     lhsT_scale=w4_q[1][:, P * n:P * (n + 1)],
                     rhs=quantised[0][:].bitcast(FP8X4), rhs_scale=quantised[1][:], start=True, stop=True)
-                bent = ring.tile([P, PAGE_CHUNKS[c]], F32, name="bent", bufs=6)
-                nc.scalar.activation(out=bent[:], in_=acc[:], func=ACT.Tanh)
-                nc.vector.tensor_scalar(out=bent[:], in0=bent[:], scalar1=outw_t[:, n:n + 1], scalar2=None,
-                                        op0=ALU.mult)
-                nc.sync.dma_start(out=out_rows[:, n, cols], in_=bent[:])
+                nc.scalar.activation(out=result[:, n, :], in_=acc[:], func=ACT.Tanh)
+                nc.vector.tensor_scalar(out=result[:, n, :], in0=result[:, n, :], scalar1=outw_t[:, n:n + 1],
+                                        scalar2=None, op0=ALU.mult)
+                nc.sync.dma_start(out=out_rows[:, n, cols], in_=result[:, n, :])
 
         chunks = len(PAGE_CHUNKS)
-        weave(nc.vector.tensor_copy, PACK - 1, 0)
-        waiting = None
+        vector_chunks = chunks - SCALAR_TAIL_CHUNKS
+        for c in range(vector_chunks, chunks):
+            weave(nc.scalar.copy, LAST, c)
+        weave(nc.vector.tensor_copy, LAST, 0)
+        page_q = []
         for c in range(chunks):
-            if c + 1 < chunks:
-                weave(nc.vector.tensor_copy, PACK - 1, c + 1)
-            codes = held([P, PAGE_CHUNKS[c]], U32, f"page_codes{c}")
-            scales = held([P, PAGE_CHUNKS[c]], U8, f"page_scales{c}")
-            nc.vector.quantize_mx(out=codes[:].bitcast(FP8X4), scales=scales[:],
-                                  in_=woven[c][:].rearrange("p c i -> p (c i)"))
-            if waiting is not None:
-                score(c - 1, waiting)
-            waiting = (codes, scales)
-        score(chunks - 1, waiting)
+            if c + 1 < vector_chunks:
+                weave(nc.vector.tensor_copy, LAST, c + 1)
+            page_q.append(quantise(woven[c][:].rearrange("p c i -> p (c i)"), PAGE_CHUNKS[c], f"page{c}"))
+            if c > 0:
+                score(c - 1, page_q[c - 1])
+        score(chunks - 1, page_q[chunks - 1])

from contextlib import ExitStack

import concourse.mybir as mybir

K, M, H, N, T, S, PAIRS = 1024, 512, 512, 384, 2048, 1024, 512
FLOPS = 2 * (K * H * S + M * H * S + K * H * S + H * N * T)

F32 = mybir.dt.float32
BF16 = mybir.dt.bfloat16
I32 = mybir.dt.int32
U32 = mybir.dt.uint32
U16 = mybir.dt.uint16
U8 = mybir.dt.uint8
FP8X4 = mybir.dt.float8_e4m3fn_x4
FP4X4 = mybir.dt.float4_e2m1fn_x4
ALU = mybir.AluOpType
ACT = mybir.ActivationFunctionType

P = 128
PACK = 4
QUADRANTS = 4
PER_COLUMN = 16
PASS = P * PACK
HALF = 512
PIECE = 256
N_TILES = N // P
LAST = PACK - 1
PAGE_CHUNKS = (256, 512, 256, 512, 256, 256)
SCALAR_TAIL_CHUNKS = 2


def tile_list_water_rights_exchange_kernel(
    tc, tab_words, tab_scales, offs, offs2, offs3, offs4, w1, w2, canal, w3_words, w3_scales,
    gain, wgs, page0, ask, w4, outw, out,
):
    nc = tc.nc
    with ExitStack() as ctx:
        lists = ctx.enter_context(tc.tile_pool(name="lists", bufs=1))
        keep = ctx.enter_context(tc.tile_pool(name="keep", bufs=1))
        shared = ctx.enter_context(tc.tile_pool(name="shared", bufs=1))
        ring = ctx.enter_context(tc.tile_pool(name="ring", bufs=2))
        psum = ctx.enter_context(tc.psum_pool(name="psum", bufs=4))

        def held(shape, dtype, name, tag=""):
            return keep.tile(shape, dtype, name=name, tag=tag or name, align_bytes=64)

        pick = lists.tile([P, S // PER_COLUMN], U16, name="pick")
        put = lists.tile([P, S // PER_COLUMN], U16, name="put")
        sellers = lists.tile([P, PAIRS // PER_COLUMN], U16, name="sellers")
        buyers = lists.tile([P, PAIRS // PER_COLUMN], U16, name="buyers")

        tab_w = [held([P, T], U32, f"tab_w{a}") for a in range(2)]
        tab_s = held([P, T], U8, "tab_s")
        w3_s_raw = held([P, 2, H], U8, "w3_s_raw")
        v_s1 = held([P, S], U8, "v_s1")
        nc.gpsimd.memset(tab_s[:].bitcast(I32), 0)
        nc.gpsimd.memset(w3_s_raw[:].rearrange("p a c -> p (a c)").bitcast(I32), 0)
        nc.gpsimd.memset(v_s1[:].bitcast(I32), 0)
        gain_t = held([P, PACK], F32, "gain_t")
        ask_t = held([P, PACK], F32, "ask_t")
        outw_t = held([P, N_TILES], F32, "outw_t")

        w1_raw = [held([P, PACK, H], F32, f"w1_raw{a}") for a in range(2)]
        w2_raw = held([P, PACK, H], F32, "w2_raw")
        w3_w_raw = held([P, 2, 2 * H], U8, "w3_w_raw")
        canal_raw = [held([P, PACK, PIECE], F32, f"canal_raw{c}") for c in range(S // PIECE)]
        wgs_dealt = shared.tile([P, PACK, S], F32, name="wgs_dealt", offset=0, align_bytes=64)
        page = [held([P, T], F32, f"page{t}") for t in range(PACK)]
        w4_raw = held([P, PACK, N], F32, "w4_raw")

        canal_rows = canal.rearrange("(p i) j -> p i j", i=PACK)
        page_rows = page0.rearrange("(p t) c -> p t c", t=PACK)
        wgs_rows = wgs.rearrange("(b t) j -> b t j", t=PACK)

        def load_words(a):
            nc.sync.dma_start(out=tab_w[a][:].bitcast(I32),
                              in_=tab_words[a].rearrange("p t i -> p (t i)").bitcast(I32))

        def load_w1(a):
            nc.sync.dma_start(out=w1_raw[a][:],
                              in_=w1[PASS * a:PASS * (a + 1), :].rearrange("(p i) c -> p i c", i=PACK))

        def load_wgs(first, end):
            for q in range(QUADRANTS):
                nc.sync.dma_start(out=wgs_dealt[32 * q:32 * (q + 1), first:end, :], in_=wgs_rows[:, first:end, :])

        def load_page(t):
            nc.sync.dma_start(out=page[t][:], in_=page_rows[:, t, :])

        v_w = [[held([P, HALF], U32, f"v_w{a}_{h}") for h in range(2)] for a in range(2)]
        v_s = held([P, S], U8, "v_s")
        v_planes = [v_s, v_s1]

        def entries(offsets, first, end):
            return offsets[:, first // PER_COLUMN:end // PER_COLUMN]

        def gather_words(a, h):
            nc.vector.tensor_copy(v_w[a][h][:], tab_w[a][:].indirect(entries(pick, HALF * h, HALF * (h + 1))))

        nc.sync.dma_start(pick[:], offs)
        nc.sync.dma_start(out=w3_w_raw[:].bitcast(I32), in_=w3_words.rearrange("a p c -> p a c").bitcast(I32))
        for q in range(QUADRANTS):
            nc.sync.dma_start(out=tab_s[32 * q:32 * q + 8, :].bitcast(I32),
                              in_=tab_scales[:, 4 * q:4 * q + 4, :].bitcast(I32))
        load_words(0)
        load_words(1)
        load_w1(0)
        for q in range(QUADRANTS):
            nc.sync.dma_start(out=w3_s_raw[32 * q:32 * q + 4, :, :].bitcast(I32),
                              in_=w3_scales[:, 4 * q:4 * q + 4, :].rearrange("a e c -> e a c").bitcast(I32))
        load_w1(1)
        w3_w = held([P, 2, 2 * H], U8, "w3_w")
        w3_s = held([P, 2, H], U8, "w3_s")
        nc.vector.tensor_copy(out=w3_w[:].bitcast(U16).rearrange("p a (t m) -> p a m t", t=PACK),
                              in_=w3_w_raw[:].bitcast(U16).rearrange("p a (m t) -> p a m t", t=PACK))
        nc.vector.tensor_copy(v_s[:], tab_s[:].indirect(pick[:]))
        for q in range(QUADRANTS):
            nc.sync.dma_start(out=v_s1[32 * q:32 * q + 4, :].bitcast(I32),
                              in_=v_s[32 * q + 4:32 * q + 8, :].bitcast(I32))
        nc.sync.dma_start(out=w2_raw[:], in_=w2.rearrange("(p i) c -> p i c", i=PACK))
        gather_words(0, 0)
        nc.sync.dma_start(put[:], offs2)
        nc.sync.dma_start(out=gain_t[:], in_=gain.rearrange("(p t) -> p t", t=PACK))
        for c in range(S // PIECE):
            nc.sync.dma_start(out=canal_raw[c][:], in_=canal_rows[:, :, PIECE * c:PIECE * (c + 1)])
        load_wgs(0, 1)
        load_page(0)
        load_wgs(1, 2)
        load_page(1)
        nc.sync.dma_start(sellers[:], offs3)
        nc.sync.dma_start(buyers[:], offs4)
        nc.sync.dma_start(out=ask_t[:], in_=ask.rearrange("(p t) -> p t", t=PACK))
        load_wgs(2, PACK)
        nc.sync.dma_start(out=w4_raw[:], in_=w4.rearrange("(p i) n -> p i n", i=PACK))
        load_page(2)
        load_page(3)
        nc.sync.dma_start(out=outw_t[:], in_=outw.rearrange("(p c) -> p c", c=N_TILES))

        nc.gpsimd.tensor_copy(out=w3_s[:].rearrange("p a (t m) -> p a t m", t=PACK),
                              in_=w3_s_raw[:].rearrange("p a (m t) -> p a t m", t=PACK))
        gather_words(1, 0)

        def quantise(grouped, width, name):
            codes = held([P, width], U32, name + "_codes")
            scales = held([P, width], U8, name + "_scales")
            nc.vector.quantize_mx(out=codes[:].bitcast(FP8X4), scales=scales[:], in_=grouped)
            return codes, scales

        def round_weight(copy, raw, groups, name):
            grouped = held([P, raw.shape[2] * PACK], BF16, name + "_bf16")
            copy(out=grouped[:].rearrange("p (t m i) -> p m i t", t=groups, i=PACK),
                 in_=raw[:].rearrange("p i (m t) -> p m i t", t=groups))
            return grouped[:]

        def round_canal(copy, c):
            grouped = held([P, PIECE * PACK], BF16, f"canal{c}_bf16")
            copy(out=grouped[:].rearrange("p (c e i) -> p c i e", e=4, i=PACK),
                 in_=canal_raw[c][:].rearrange("p i (c e) -> p c i e", e=4))
            return grouped[:]

        w1_b = [round_weight(nc.scalar.copy, w1_raw[a], PACK, f"w1_{a}") for a in range(2)]
        w1_q = [quantise(w1_b[0], H, "w1_0")]
        w2_b = round_weight(nc.vector.tensor_copy, w2_raw, PACK, "w2")
        w1_q.append(quantise(w1_b[1], H, "w1_1"))
        canal_b = [round_canal(nc.vector.tensor_copy, 0)]
        w2_q = quantise(w2_b, H, "w2")
        canal_q = [quantise(canal_b[0], PIECE, "canal0")]

        top = [held([P, S], F32, f"top{t}") for t in range(PACK)]
        weight = [held([P, S], F32, f"weight{t}") for t in range(PACK)]

        def top_half(t, h):
            return top[t][:, HALF * h:HALF * (h + 1)]

        def second_sum(t, h):
            acc = psum.tile([P, HALF], F32, name="acc_scalar")
            for a in range(2):
                nc.tensor.matmul_mx(
                    out=acc[:], lhsT=w3_w[:, a, 2 * P * t:2 * P * (t + 1)].bitcast(FP4X4),
                    lhsT_scale=w3_s[:, a, P * t:P * (t + 1)],
                    rhs=v_w[a][h][:].bitcast(FP8X4), rhs_scale=v_planes[a][:, HALF * h:HALF * (h + 1)],
                    start=(a == 0), stop=(a == 1))
            nc.scalar.copy(out=top_half(t, h), in_=acc[:])

        def larger(t, h, into):
            acc = psum.tile([P, HALF], F32, name="acc_first")
            rows = slice(P * t, P * (t + 1))
            for e in range(HALF // PIECE):
                cols = slice(PIECE * e, PIECE * (e + 1))
                c = (HALF // PIECE) * h + e
                for a in range(2):
                    nc.tensor.matmul_mx(
                        out=acc[:, cols], lhsT=w1_q[a][0][:, rows].bitcast(FP8X4), lhsT_scale=w1_q[a][1][:, rows],
                        rhs=v_w[a][h][:, cols].bitcast(FP8X4), rhs_scale=v_planes[a][:, PIECE * c:PIECE * (c + 1)],
                        start=(a == 0), stop=False)
                nc.tensor.matmul_mx(
                    out=acc[:, cols], lhsT=w2_q[0][:, rows].bitcast(FP8X4), lhsT_scale=w2_q[1][:, rows],
                    rhs=canal_q[c][0][:].bitcast(FP8X4), rhs_scale=canal_q[c][1][:], start=False, stop=True)
            nc.vector.tensor_tensor(out=into, in0=acc[:], in1=top_half(t, h), op=ALU.max)

        def place(t, h, values):
            nc.vector.tensor_tensor(page[t][:].indirect(entries(put, HALF * h, HALF * (h + 1))),
                                    values, weight[t][:, HALF * h:HALF * (h + 1)], ALU.mult)

        def weigh(t):
            nc.scalar.activation(out=weight[t][:], in_=wgs_dealt[:, t, :], func=ACT.Copy, scale=gain_t[:, t:t + 1])

        canal_b.append(round_canal(nc.vector.tensor_copy, 1))
        gather_words(0, 1)
        gather_words(1, 1)
        canal_q.append(quantise(canal_b[1], PIECE, "canal1"))
        canal_b.append(round_canal(nc.scalar.copy, 2))
        canal_b.append(round_canal(nc.scalar.copy, 3))
        weigh(0)
        for h in range(2):
            for t in range(PACK):
                second_sum(t, h)
        larger(0, 0, top_half(0, 0))
        canal_q.append(quantise(canal_b[2], PIECE, "canal2"))
        larger(1, 0, top_half(1, 0))
        canal_q.append(quantise(canal_b[3], PIECE, "canal3"))
        larger(2, 0, top_half(2, 0))
        larger(3, 0, top_half(3, 0))
        place(0, 0, top_half(0, 0))
        larger(0, 1, top_half(0, 1))
        larger(1, 1, top_half(1, 1))
        place(0, 1, top_half(0, 1))
        larger(2, 1, top_half(2, 1))
        for t in range(1, PACK):
            weigh(t)
        w4_b = round_weight(nc.scalar.copy, w4_raw, N_TILES, "w4")

        chunk_start = [sum(PAGE_CHUNKS[:c]) for c in range(len(PAGE_CHUNKS))]
        woven = [shared.tile([P, w, PACK], BF16, name=f"woven{c}", offset=2 * PACK * chunk_start[c], align_bytes=64)
                 for c, w in enumerate(PAGE_CHUNKS)]

        def weave(copy, t, c):
            copy(out=woven[c][:, :, t], in_=page[t][:, chunk_start[c]:chunk_start[c] + PAGE_CHUNKS[c]])

        def fetch(t):
            sell = ring.tile([P, PAIRS], F32, name="sell")
            buy = ring.tile([P, PAIRS], F32, name="buy")
            nc.vector.tensor_copy(sell[:], page[t][:].indirect(sellers[:]))
            nc.vector.tensor_copy(buy[:], page[t][:].indirect(buyers[:]))
            return sell, buy

        def settle_buyers(t, pair, low):
            sell, buy = pair
            nc.vector.tensor_tensor(page[t][:].indirect(buyers[:]), sell[:], buy[:], ALU.add)
            nc.vector.scalar_tensor_tensor(out=low[:], in0=sell[:], scalar=ask_t[:, t:t + 1], in1=buy[:],
                                           op0=ALU.add, op1=ALU.min)

        def settle_sellers(t, low):
            nc.vector.tensor_copy(page[t][:].indirect(sellers[:]), low[:])

        def weave_on_scalar(t):
            for c in range(len(PAGE_CHUNKS)):
                weave(nc.scalar.copy, t, c)

        for t in range(LAST - 1):
            pair = fetch(t)
            place(t + 1, 0, top_half(t + 1, 0))
            low = ring.tile([P, PAIRS], F32, name="low")
            settle_buyers(t, pair, low)
            place(t + 1, 1, top_half(t + 1, 1))
            settle_sellers(t, low)
            weave_on_scalar(t)
        w4_q = quantise(w4_b, N, "w4")

        pair = fetch(LAST - 1)
        place(LAST, 0, top_half(LAST, 0))
        low = held([P, PAIRS], F32, "low_before_last")
        settle_buyers(LAST - 1, pair, low)
        settle_sellers(LAST - 1, low)
        weave_on_scalar(LAST - 1)
        top_last = held([P, HALF], F32, "top_last", tag="low_before_last")
        larger(LAST, 1, top_last[:])
        place(LAST, 1, top_last[:])

        pair = fetch(LAST)
        low = held([P, PAIRS], F32, "low_last", tag=f"page{LAST - 1}")
        settle_buyers(LAST, pair, low)
        settle_sellers(LAST, low)

        out_rows = out.rearrange("(p c) t -> p c t", c=N_TILES)
        spent = ("w1_raw0", "w1_raw1", "w2_raw", "page0", "page1", "w4_raw")

        def score(c, quantised):
            cols = slice(chunk_start[c], chunk_start[c] + PAGE_CHUNKS[c])
            result = held([P, N_TILES, PAGE_CHUNKS[c]], F32, f"result{c}", tag=spent[c])
            for n in range(N_TILES):
                acc = psum.tile([P, PAGE_CHUNKS[c]], F32, name="acc_scalar")
                nc.tensor.matmul_mx(
                    out=acc[:], lhsT=w4_q[0][:, P * n:P * (n + 1)].bitcast(FP8X4),
                    lhsT_scale=w4_q[1][:, P * n:P * (n + 1)],
                    rhs=quantised[0][:].bitcast(FP8X4), rhs_scale=quantised[1][:], start=True, stop=True)
                nc.scalar.activation(out=result[:, n, :], in_=acc[:], func=ACT.Tanh)
                nc.vector.tensor_scalar(out=result[:, n, :], in0=result[:, n, :], scalar1=outw_t[:, n:n + 1],
                                        scalar2=None, op0=ALU.mult)
                nc.sync.dma_start(out=out_rows[:, n, cols], in_=result[:, n, :])

        chunks = len(PAGE_CHUNKS)
        vector_chunks = chunks - SCALAR_TAIL_CHUNKS
        for c in range(vector_chunks, chunks):
            weave(nc.scalar.copy, LAST, c)
        weave(nc.vector.tensor_copy, LAST, 0)
        page_q = []
        for c in range(chunks):
            if c + 1 < vector_chunks:
                weave(nc.vector.tensor_copy, LAST, c + 1)
            page_q.append(quantise(woven[c][:].rearrange("p c i -> p (c i)"), PAGE_CHUNKS[c], f"page{c}"))
            if c > 0:
                score(c - 1, page_q[c - 1])
        score(chunks - 1, page_q[chunks - 1])
